import numpy as np
import ml_dtypes


def mxq(x, axis, fmt="e4m3"):
    dtype, down = {"e4m3": (ml_dtypes.float8_e4m3fn, 7), "e5m2": (ml_dtypes.float8_e5m2, 14)}[fmt]
    v = np.moveaxis(np.asarray(x, np.float32).astype(ml_dtypes.bfloat16).astype(np.float64), axis, -1)
    blocks = v.reshape(v.shape[:-1] + (-1, 32))
    amax = np.abs(blocks).max(-1, keepdims=True)
    byte = np.maximum(np.where(amax > 0, np.frexp(amax)[1] - 1 + 127, 0) - down, 1)
    scale = np.exp2(byte - 127.0)
    codes = (blocks / scale).astype(np.float32).astype(dtype).astype(np.float64)
    return np.moveaxis((codes * scale).reshape(v.shape), -1, axis)


WIDE = False


def mx_kscale(k):
    if not WIDE:
        return np.ones(k)
    levels = np.array([10, -10, 5, -5, 0])
    if k % 512:
        return np.exp2(np.random.permutation(np.resize(levels, k // 32))).repeat(32)
    a = np.empty((k // 512, 16))
    for p in range(k // 512):
        a[p, :8] = np.random.permutation(np.resize(levels, 8))
        for g in range(8):
            far = levels[np.abs(levels - a[p, g]) >= 10]
            a[p, g + 8] = far[np.random.randint(len(far))]
    return np.exp2(a.ravel()).repeat(32)


def f64(x):
    return np.asarray(x).astype(np.float64)


def striped(idx):
    return np.tile(idx.reshape(-1, 16).T, (8, 1)).astype(np.uint16)


def unstriped(offs):
    return offs[:16].T.reshape(-1).astype(np.int64)


E2M1 = np.array([0.0, 0.5, 1.0, 1.5, 2.0, 3.0, 4.0, 6.0, -0.0, -0.5, -1.0, -1.5, -2.0, -3.0, -4.0, -6.0])


def pack_weight(w, fmt):
    k, n = w.shape
    w = f64(np.asarray(w, np.float32).astype(ml_dtypes.bfloat16)).reshape(k // 32, 32, n)
    amax = np.abs(w).max(1)
    if fmt == "e4m3":
        byte = np.frexp(amax)[1] - 1 + 127 - 7
    else:
        mant, ex = np.frexp(amax / 6.0)
        byte = np.where(mant > 0.5, ex, ex - 1) + 127
    byte = np.clip(np.where(amax > 0, byte, 1), 1, 254)
    scaled = (w * np.exp2(127.0 - byte)[:, None, :]).reshape(k, n).astype(np.float32)
    by_word = np.ascontiguousarray(scaled.reshape(k // 512, 128, 4, n).transpose(0, 1, 3, 2))
    if fmt == "e4m3":
        words = by_word.astype(ml_dtypes.float8_e4m3fn).view(np.uint8)
    else:
        c = by_word.astype(ml_dtypes.float4_e2m1fn).view(np.uint8) & 0xF
        words = (c[..., 0::2] | (c[..., 1::2] << 4)).reshape(k // 512, 128, 2 * n)
    return np.ascontiguousarray(words), np.ascontiguousarray(byte.astype(np.uint8).reshape(k // 512, 16, n))


def unpack_weight(words, scales, fmt):
    g, _, n = scales.shape
    words = np.ascontiguousarray(words).reshape(g, 128, n, -1)
    if fmt == "e4m3":
        vals = words.view(ml_dtypes.float8_e4m3fn).astype(np.float64)
    else:
        nib = np.empty((g, 128, n, 4), np.uint8)
        nib[..., 0::2] = words & 0xF
        nib[..., 1::2] = words >> 4
        vals = E2M1[nib]
    vals = vals * np.repeat(np.exp2(scales.astype(np.float64) - 127.0), 8, axis=1)[..., None]
    return vals.transpose(0, 1, 3, 2).reshape(g * 512, n)


def gelu(v):
    return 0.5 * v * (1.0 + np.tanh(np.sqrt(2.0 / np.pi) * (v + 0.044715 * v**3)))


K, H, T, S, T2, S2, T3 = 1536, 1024, 2048, 1024, 2048, 512, 2048


def setup_inputs():
    n = np.random.standard_normal
    s = mx_kscale(K)[:, None]
    u = mx_kscale(H)[:, None]
    tab_words, tab_scales = pack_weight(n((K, T)) * s, "e4m3")
    tab2_words, tab2_scales = pack_weight(n((H, T3)) / np.sqrt(H) / u, "e4m3")
    w4_words, w4_scales = pack_weight(n((K, H)) / np.sqrt(K) / s * u.T, "e2m1")
    return {
        "tab_words": tab_words, "tab_scales": tab_scales,
        "tab2_words": tab2_words, "tab2_scales": tab2_scales,
        "w4_words": w4_words, "w4_scales": w4_scales,
        "floor_m": (n((H, S)) * u).astype(np.float32),
        "sit": (0.8 * n((H, S)) * u).astype(np.float32),
        "expo": np.exp(0.4 * n((S2, S))).astype(np.float32),
        "page1": (0.7 * n((S2, T2))).astype(np.float32),
        "wgo": np.exp(0.3 * n((128, S))).astype(np.float32),
        "offs": striped(np.random.permutation(T)[:S]),
        "offs2": striped(np.random.permutation(T3)[:S2]),
        "offs3": striped(np.random.permutation(T2)[:S]),
    }


def reference(tab_words, tab_scales, tab2_words, tab2_scales, w4_words, w4_scales,
              floor_m, sit, expo, page1, wgo, offs, offs2, offs3):
    v = unpack_weight(tab_words, tab_scales, "e4m3")[:, unstriped(offs)]
    v2 = unpack_weight(tab2_words, tab2_scales, "e4m3")[:, unstriped(offs2)]
    w4 = unpack_weight(w4_words, w4_scales, "e2m1")
    h = np.maximum(w4.T @ v, f64(floor_m))
    hq = mxq(h, 0, "e4m3")
    sq = mxq(f64(sit), 0, "e4m3")
    e = v2.T @ hq + v2.T @ sq
    y = np.tanh(f64(expo) * e)
    out = f64(page1).copy()
    out[:, unstriped(offs3)] = np.tile(f64(wgo), (S2 // 128, 1)) * y
    return out

@@ -1,0 +1,238 @@
+from contextlib import ExitStack
+
+import concourse.mybir as mybir
+
+K, H, T, S, T2, S2, T3 = 1536, 1024, 2048, 1024, 2048, 512, 2048
+FLOPS = 2 * K * H * S + 2 * 2 * H * S2 * S
+
+F32 = mybir.dt.float32
+BF16 = mybir.dt.bfloat16
+I32 = mybir.dt.int32
+U32 = mybir.dt.uint32
+U16 = mybir.dt.uint16
+U8 = mybir.dt.uint8
+FP8X4 = mybir.dt.float8_e4m3fn_x4
+FP4X4 = mybir.dt.float4_e2m1fn_x4
+ALU = mybir.AluOpType
+ACT = mybir.ActivationFunctionType
+
+P = 128
+PACK = 4
+KP = P * PACK
+A1 = K // KP
+A2 = H // KP
+HALF = 512
+NH = S // HALF
+MB = S2 // P
+JB = 128
+QUAD = 32
+LIVE = 4
+TS0 = QUAD - A1 * LIVE
+PLANE_ROWS = 3 * QUAD + LIVE
+
+
+def tile_list_item_equating_scores_kernel(tc, tab_words, tab_scales, tab2_words, tab2_scales,
+                                                    w4_words, w4_scales, floor_m, sit, expo, page1, wgo,
+                                                    offs, offs2, offs3, out):
+    nc = tc.nc
+    with ExitStack() as ctx:
+        keep = ctx.enter_context(tc.tile_pool(name="keep", bufs=1))
+        ring = ctx.enter_context(tc.tile_pool(name="ring", bufs=2))
+        psum1 = ctx.enter_context(tc.psum_pool(name="psum1", bufs=6))
+        psum2 = ctx.enter_context(tc.psum_pool(name="psum2", bufs=2))
+
+        idx1 = keep.tile([P, S // 16], U16, name="idx1")
+        idx2 = keep.tile([P, S2 // 16], U16, name="idx2")
+        idx3 = keep.tile([P, S // 16], U16, name="idx3")
+        tab = [keep.tile([P, T], I32, name="tab%d" % a) for a in range(A1)]
+        tab2 = [keep.tile([P, T3], I32, name="tab2_%d" % a) for a in range(A2)]
+        tab_sc = keep.tile([P, T], U8, name="tab_sc")
+        tab2_sc = keep.tile([P, T3], U8, name="tab2_sc")
+        v = {(a, h): keep.tile([P, HALF], U32, name="v%d_%d" % (a, h), align_bytes=64)
+             for a in range(A1) for h in range(NH)}
+        v_sc_packed = keep.tile([P, S], U8, name="v_sc_packed")
+        v_sc = keep.tile([P, A1 * S], U8, name="v_sc", align_bytes=64)
+        v2 = [keep.tile([P, S2], U32, name="v2_%d" % a, align_bytes=64) for a in range(A2)]
+        v2_sc = keep.tile([P, S2], U8, name="v2_sc", align_bytes=64)
+        w_raw = keep.tile([P, A1 * 2 * H], U8, name="w_raw")
+        w_sc_raw = keep.tile([P, A1 * H], U8, name="w_sc_raw")
+        w = [keep.tile([P, A1 * 2 * KP], U8, name="w%d" % b, align_bytes=64) for b in range(A2)]
+        w_sc = [keep.tile([P, A1 * KP], U8, name="w_sc%d" % b, align_bytes=64) for b in range(A2)]
+        page = [keep.tile([P, T2], F32, name="page%d" % m) for m in range(MB)]
+        wg = [keep.tile([P, HALF], F32, name="wg%d" % h) for h in range(NH)]
+        ex = {}
+        fl = {}
+        st = {}
+        hq = {}
+        sq = {}
+        y = {}
+
+        def words(src, a):
+            return src[a].rearrange("p t i -> p (t i)").bitcast(I32)
+
+        def load_rows(src, tag, h, b):
+            t = ring.tile([P, PACK, HALF], F32, name=tag, tag=tag)
+            rows = src[b * KP:(b + 1) * KP, h * HALF:(h + 1) * HALF]
+            nc.sync.dma_start(out=t[:], in_=rows.rearrange("(p t) j -> p t j", t=PACK))
+            return t
+
+        def load_expo(h, m):
+            ex[h, m] = keep.tile([P, HALF], F32, name="ex%d_%d" % (h, m))
+            nc.sync.dma_start(out=ex[h, m][:], in_=expo[m * P:(m + 1) * P, h * HALF:(h + 1) * HALF])
+
+        def load_page(m):
+            nc.sync.dma_start(out=page[m][:], in_=page1[m * P:(m + 1) * P, :])
+
+        def load_wgo(h):
+            nc.sync.dma_start(out=wg[h][:], in_=wgo[:, h * HALF:(h + 1) * HALF])
+
+        def quantise(staged, tag):
+            codes = ring.tile([P, HALF], U32, name=tag + "_codes", tag=tag + "_codes", bufs=4, align_bytes=64)
+            scales = ring.tile([P, HALF], U8, name=tag + "_scales", tag=tag + "_scales", bufs=4, align_bytes=64)
+            nc.vector.quantize_mx(out=codes[:].bitcast(FP8X4), scales=scales[:], in_=staged[:])
+            return codes, scales
+
+        def features(h, b):
+            staged = ring.tile([P, HALF * PACK], BF16, name="h_bf", tag="h_bf", align_bytes=64)
+            for jb in range(HALF // JB):
+                j0 = h * HALF + jb * JB
+                acc = psum1.tile([P, PACK, JB], F32, name="acc1", tag="acc1")
+                for t in range(PACK):
+                    for a in range(A1):
+                        c0 = a * KP + t * P
+                        nc.tensor.matmul_mx(
+                            out=acc[:, t, :],
+                            lhsT=w[b][:, 2 * c0:2 * (c0 + P)].bitcast(FP4X4),
+                            lhsT_scale=w_sc[b][:, c0:c0 + P],
+                            rhs=v[a, h][:, jb * JB:(jb + 1) * JB].bitcast(FP8X4),
+                            rhs_scale=v_sc[:, a * S + j0:a * S + j0 + JB],
+                            start=(a == 0), stop=(a == A1 - 1))
+                nc.vector.tensor_tensor(
+                    out=staged[:, jb * JB * PACK:(jb + 1) * JB * PACK].rearrange("p (c i t) -> p c t i", i=2, t=PACK),
+                    in0=acc[:].rearrange("p t (c i) -> p c t i", i=2),
+                    in1=fl[h, b][:, :, jb * JB:(jb + 1) * JB].rearrange("p t (c i) -> p c t i", i=2),
+                    op=ALU.max)
+            hq[h, b] = quantise(staged, "hq")
+
+        def sitting(h, b):
+            staged = ring.tile([P, HALF * PACK], BF16, name="s_bf", tag="s_bf", align_bytes=64)
+            nc.scalar.copy(
+                out=staged[:].rearrange("p (c i t) -> p c t i", i=2, t=PACK),
+                in_=st[h, b][:].rearrange("p t (c i) -> p c t i", i=2))
+            sq[h, b] = quantise(staged, "sq")
+
+        def scores(h, m):
+            acc = psum2.tile([P, HALF], F32, name="acc2", tag="acc2")
+            passes = [(q, b) for b in range(A2) for q in (hq, sq)]
+            for n, (q, b) in enumerate(passes):
+                codes, scales = q[h, b]
+                nc.tensor.matmul_mx(
+                    out=acc[:],
+                    lhsT=v2[b][:, m * P:(m + 1) * P].bitcast(FP8X4),
+                    lhsT_scale=v2_sc[LIVE * b:, m * P:(m + 1) * P],
+                    rhs=codes[:].bitcast(FP8X4),
+                    rhs_scale=scales[:],
+                    start=(n == 0), stop=(n == len(passes) - 1))
+            z = ring.tile([P, HALF], F32, name="z", tag="z", bufs=3)
+            nc.vector.tensor_tensor(out=z[:], in0=acc[:], in1=ex[h, m][:], op=ALU.mult)
+            y[h, m] = keep.tile([P, HALF], F32, name="y%d_%d" % (h, m))
+            nc.scalar.activation(out=y[h, m][:], in_=z[:], func=ACT.Tanh)
+
+        def entries(h):
+            return slice(h * HALF // 16, (h + 1) * HALF // 16)
+
+        def put(h, m):
+            nc.vector.tensor_tensor(out=page[m][:].indirect(idx3[:, entries(h)]), in0=y[h, m][:], in1=wg[h][:],
+                                    op=ALU.mult)
+
+        for q in range(P // QUAD):
+            nc.vector.memset(tab_sc[q * QUAD:q * QUAD + TS0, :].bitcast(I32), 0)
+        nc.vector.memset(w_sc_raw[:].bitcast(I32), 0)
+        nc.vector.memset(v_sc[3 * QUAD:, :].bitcast(I32), 0)
+        nc.vector.memset(tab2_sc[:].bitcast(I32), 0)
+
+        nc.sync.dma_start(idx1[:], offs)
+        for q in range(P // QUAD):
+            nc.scalar.dma_start(out=tab_sc[q * QUAD + TS0:(q + 1) * QUAD, :].bitcast(I32),
+                                in_=tab_scales[:, LIVE * q:LIVE * (q + 1), :].bitcast(I32))
+        nc.sync.dma_start(out=tab[0][:], in_=words(tab_words, 0))
+        nc.sync.dma_start(out=tab[1][:], in_=words(tab_words, 1))
+        for q in range(P // QUAD):
+            nc.sync.dma_start(
+                out=w_sc_raw[q * QUAD:q * QUAD + LIVE, :].bitcast(I32).rearrange("r (a n) -> r a n", a=A1),
+                in_=w4_scales[:, LIVE * q:LIVE * (q + 1), :].bitcast(I32).rearrange("a r n -> r a n"))
+        nc.sync.dma_start(out=w_raw[:].bitcast(I32).rearrange("p (a n) -> p a n", a=A1),
+                          in_=w4_words.bitcast(I32).rearrange("a p n -> p a n"))
+        nc.sync.dma_start(out=tab[2][:], in_=words(tab_words, 2))
+
+        nc.vector.tensor_copy(out=v_sc_packed[:], in_=tab_sc[:].indirect(idx1[:]))
+        for a in range(A1):
+            s0 = TS0 + LIVE * a
+            nc.scalar.dma_start(out=v_sc[:PLANE_ROWS, a * S:(a + 1) * S].bitcast(I32),
+                                in_=v_sc_packed[s0:s0 + PLANE_ROWS, :].bitcast(I32))
+        for h in range(NH):
+            for a in range(A1):
+                nc.vector.tensor_copy(out=v[a, h][:], in_=tab[a][:].bitcast(U32).indirect(idx1[:, entries(h)]))
+
+        for b in range(A2):
+            nc.gpsimd.tensor_copy(
+                out=w_sc[b][:].rearrange("p (a t m) -> p a t m", a=A1, t=PACK),
+                in_=w_sc_raw[:].rearrange("p (a b m t) -> p b a t m", a=A1, b=A2, t=PACK)[:, b])
+            nc.scalar.copy(
+                out=w[b][:].bitcast(U16).rearrange("p (a t m) -> p a t m", a=A1, t=PACK),
+                in_=w_raw[:].bitcast(U16).rearrange("p (a b m t) -> p b a t m", a=A1, b=A2, t=PACK)[:, b])
+
+        for b in range(A2):
+            fl[0, b] = load_rows(floor_m, "fl", 0, b)
+        for b in range(A2):
+            st[0, b] = load_rows(sit, "st", 0, b)
+        nc.sync.dma_start(idx2[:], offs2)
+        for q in range(P // QUAD):
+            nc.sync.dma_start(out=tab2_sc[q * QUAD:q * QUAD + A2 * LIVE, :].bitcast(I32),
+                              in_=tab2_scales[:, LIVE * q:LIVE * (q + 1), :].bitcast(I32))
+        for a in range(A2):
+            nc.sync.dma_start(out=tab2[a][:], in_=words(tab2_words, a))
+        nc.sync.dma_start(idx3[:], offs3)
+        load_expo(0, 0)
+        load_expo(0, 1)
+        load_wgo(0)
+        load_page(0)
+
+        for b in range(A2):
+            features(0, b)
+        for b in range(A2):
+            sitting(0, b)
+        nc.vector.tensor_copy(out=v2_sc[:], in_=tab2_sc[:].indirect(idx2[:]))
+        for a in range(A2):
+            nc.vector.tensor_copy(out=v2[a][:], in_=tab2[a][:].bitcast(U32).indirect(idx2[:]))
+
+        load_expo(0, 2)
+        load_page(1)
+        load_expo(0, 3)
+        load_page(2)
+        for b in range(A2):
+            fl[1, b] = load_rows(floor_m, "fl", 1, b)
+        for b in range(A2):
+            st[1, b] = load_rows(sit, "st", 1, b)
+        load_page(3)
+        load_expo(1, 0)
+        load_expo(1, 1)
+        load_wgo(1)
+        load_expo(1, 2)
+        load_expo(1, 3)
+
+        scores(0, 0)
+        for m in range(MB - 1):
+            scores(0, m + 1)
+            put(0, m)
+        for b in range(A2):
+            features(1, b)
+        for b in range(A2):
+            sitting(1, b)
+        put(0, MB - 1)
+        scores(1, 0)
+        for m in range(MB):
+            if m + 1 < MB:
+                scores(1, m + 1)
+            put(1, m)
+            nc.sync.dma_start(out=out[m * P:(m + 1) * P, :], in_=page[m][:])

@@ -38,8 +38,7 @@ def tile_list_item_equating_scores_kernel(tc, tab_words, tab_scales, tab2_words,
     with ExitStack() as ctx:
         keep = ctx.enter_context(tc.tile_pool(name="keep", bufs=1))
         ring = ctx.enter_context(tc.tile_pool(name="ring", bufs=2))
-        psum1 = ctx.enter_context(tc.psum_pool(name="psum1", bufs=6))
-        psum2 = ctx.enter_context(tc.psum_pool(name="psum2", bufs=2))
+        psum = ctx.enter_context(tc.psum_pool(name="psum", bufs=1))
 
         idx1 = keep.tile([P, S // 16], U16, name="idx1")
         idx2 = keep.tile([P, S2 // 16], U16, name="idx2")
@@ -48,7 +47,7 @@ def tile_list_item_equating_scores_kernel(tc, tab_words, tab_scales, tab2_words,
         tab2 = [keep.tile([P, T3], I32, name="tab2_%d" % a) for a in range(A2)]
         tab_sc = keep.tile([P, T], U8, name="tab_sc")
         tab2_sc = keep.tile([P, T3], U8, name="tab2_sc")
-        v = {(a, h): keep.tile([P, HALF], U32, name="v%d_%d" % (a, h), align_bytes=64)
+        v = {(a, h): keep.tile([P, HALF], U32, name="picked%d_%d" % (a, h), align_bytes=64)
              for a in range(A1) for h in range(NH)}
         v_sc_packed = keep.tile([P, S], U8, name="v_sc_packed")
         v_sc = keep.tile([P, A1 * S], U8, name="v_sc", align_bytes=64)
@@ -60,6 +59,7 @@ def tile_list_item_equating_scores_kernel(tc, tab_words, tab_scales, tab2_words,
         w_sc = [keep.tile([P, A1 * KP], U8, name="w_sc%d" % b, align_bytes=64) for b in range(A2)]
         page = [keep.tile([P, T2], F32, name="page%d" % m) for m in range(MB)]
         wg = [keep.tile([P, HALF], F32, name="wg%d" % h) for h in range(NH)]
+        bank = [psum.tile([P, HALF], F32, name="bank%d" % n) for n in range(2 * MB)]
         ex = {}
         fl = {}
         st = {}
@@ -96,7 +96,7 @@ def tile_list_item_equating_scores_kernel(tc, tab_words, tab_scales, tab2_words,
             staged = ring.tile([P, HALF * PACK], BF16, name="h_bf", tag="h_bf", align_bytes=64)
             for jb in range(HALF // JB):
                 j0 = h * HALF + jb * JB
-                acc = psum1.tile([P, PACK, JB], F32, name="acc1", tag="acc1")
+                acc = bank[MB * h + jb][:].rearrange("p (t j) -> p t j", t=PACK)
                 for t in range(PACK):
                     for a in range(A1):
                         c0 = a * KP + t * P
@@ -109,7 +109,7 @@ def tile_list_item_equating_scores_kernel(tc, tab_words, tab_scales, tab2_words,
                             start=(a == 0), stop=(a == A1 - 1))
                 nc.vector.tensor_tensor(
                     out=staged[:, jb * JB * PACK:(jb + 1) * JB * PACK].rearrange("p (c i t) -> p c t i", i=2, t=PACK),
-                    in0=acc[:].rearrange("p t (c i) -> p c t i", i=2),
+                    in0=acc.rearrange("p t (c i) -> p c t i", i=2),
                     in1=fl[h, b][:, :, jb * JB:(jb + 1) * JB].rearrange("p t (c i) -> p c t i", i=2),
                     op=ALU.max)
             hq[h, b] = quantise(staged, "hq")
@@ -122,7 +122,7 @@ def tile_list_item_equating_scores_kernel(tc, tab_words, tab_scales, tab2_words,
             sq[h, b] = quantise(staged, "sq")
 
         def scores(h, m):
-            acc = psum2.tile([P, HALF], F32, name="acc2", tag="acc2")
+            acc = bank[MB * (1 - h) + m]
             passes = [(q, b) for b in range(A2) for q in (hq, sq)]
             for n, (q, b) in enumerate(passes):
                 codes, scales = q[h, b]
@@ -158,7 +158,7 @@ def tile_list_item_equating_scores_kernel(tc, tab_words, tab_scales, tab2_words,
         nc.sync.dma_start(out=tab[0][:], in_=words(tab_words, 0))
         nc.sync.dma_start(out=tab[1][:], in_=words(tab_words, 1))
         for q in range(P // QUAD):
-            nc.sync.dma_start(
+            nc.gpsimd.dma_start(
                 out=w_sc_raw[q * QUAD:q * QUAD + LIVE, :].bitcast(I32).rearrange("r (a n) -> r a n", a=A1),
                 in_=w4_scales[:, LIVE * q:LIVE * (q + 1), :].bitcast(I32).rearrange("a r n -> r a n"))
         nc.sync.dma_start(out=w_raw[:].bitcast(I32).rearrange("p (a n) -> p a n", a=A1),
@@ -188,7 +188,7 @@ def tile_list_item_equating_scores_kernel(tc, tab_words, tab_scales, tab2_words,
             st[0, b] = load_rows(sit, "st", 0, b)
         nc.sync.dma_start(idx2[:], offs2)
         for q in range(P // QUAD):
-            nc.sync.dma_start(out=tab2_sc[q * QUAD:q * QUAD + A2 * LIVE, :].bitcast(I32),
+            nc.gpsimd.dma_start(out=tab2_sc[q * QUAD:q * QUAD + A2 * LIVE, :].bitcast(I32),
                               in_=tab2_scales[:, LIVE * q:LIVE * (q + 1), :].bitcast(I32))
         for a in range(A2):
             nc.sync.dma_start(out=tab2[a][:], in_=words(tab2_words, a))
@@ -207,10 +207,9 @@ def tile_list_item_equating_scores_kernel(tc, tab_words, tab_scales, tab2_words,
             nc.vector.tensor_copy(out=v2[a][:], in_=tab2[a][:].bitcast(U32).indirect(idx2[:]))
 
         load_expo(0, 2)
-        load_page(1)
         load_expo(0, 3)
-        load_page(2)
         for b in range(A2):
+            load_page(1 + b)
             fl[1, b] = load_rows(floor_m, "fl", 1, b)
         for b in range(A2):
             st[1, b] = load_rows(sit, "st", 1, b)
@@ -222,10 +221,12 @@ def tile_list_item_equating_scores_kernel(tc, tab_words, tab_scales, tab2_words,
         load_expo(1, 3)
 
         scores(0, 0)
-        for m in range(MB - 1):
-            scores(0, m + 1)
-            put(0, m)
+        scores(0, 1)
+        put(0, 0)
+        scores(0, 2)
+        scores(0, 3)
         for b in range(A2):
+            put(0, 1 + b)
             features(1, b)
         for b in range(A2):
             sitting(1, b)

@@ -27,7 +27,7 @@ MB = S2 // P
 JB = 128
 QUAD = 32
 LIVE = 4
-TS0 = QUAD - A1 * LIVE
+BANKS = 6
 PLANE_ROWS = 3 * QUAD + LIVE
 
 
@@ -49,9 +49,8 @@ def tile_list_item_equating_scores_kernel(tc, tab_words, tab_scales, tab2_words,
         tab2_sc = keep.tile([P, T3], U8, name="tab2_sc")
         v = {(a, h): keep.tile([P, HALF], U32, name="picked%d_%d" % (a, h), align_bytes=64)
              for a in range(A1) for h in range(NH)}
-        v_sc_packed = keep.tile([P, S], U8, name="v_sc_packed")
-        v_sc = keep.tile([P, A1 * S], U8, name="v_sc", align_bytes=64)
-        v2 = [keep.tile([P, S2], U32, name="v2_%d" % a, align_bytes=64) for a in range(A2)]
+        v_sc = [keep.tile([P, S], U8, name="v_sc%d" % a, align_bytes=64) for a in range(A1)]
+        v2 = [keep.tile([P, S2], U32, name="items%d" % a, align_bytes=64) for a in range(A2)]
         v2_sc = keep.tile([P, S2], U8, name="v2_sc", align_bytes=64)
         w_raw = keep.tile([P, A1 * 2 * H], U8, name="w_raw")
         w_sc_raw = keep.tile([P, A1 * H], U8, name="w_sc_raw")
@@ -59,7 +58,7 @@ def tile_list_item_equating_scores_kernel(tc, tab_words, tab_scales, tab2_words,
         w_sc = [keep.tile([P, A1 * KP], U8, name="w_sc%d" % b, align_bytes=64) for b in range(A2)]
         page = [keep.tile([P, T2], F32, name="page%d" % m) for m in range(MB)]
         wg = [keep.tile([P, HALF], F32, name="wg%d" % h) for h in range(NH)]
-        bank = [psum.tile([P, HALF], F32, name="bank%d" % n) for n in range(2 * MB)]
+        bank = [psum.tile([P, HALF], F32, name="bank%d" % n) for n in range(BANKS)]
         ex = {}
         fl = {}
         st = {}
@@ -96,7 +95,7 @@ def tile_list_item_equating_scores_kernel(tc, tab_words, tab_scales, tab2_words,
             staged = ring.tile([P, HALF * PACK], BF16, name="h_bf", tag="h_bf", align_bytes=64)
             for jb in range(HALF // JB):
                 j0 = h * HALF + jb * JB
-                acc = bank[MB * h + jb][:].rearrange("p (t j) -> p t j", t=PACK)
+                acc = bank[(b * (HALF // JB) + jb) % BANKS][:].rearrange("p (t j) -> p t j", t=PACK)
                 for t in range(PACK):
                     for a in range(A1):
                         c0 = a * KP + t * P
@@ -105,7 +104,7 @@ def tile_list_item_equating_scores_kernel(tc, tab_words, tab_scales, tab2_words,
                             lhsT=w[b][:, 2 * c0:2 * (c0 + P)].bitcast(FP4X4),
                             lhsT_scale=w_sc[b][:, c0:c0 + P],
                             rhs=v[a, h][:, jb * JB:(jb + 1) * JB].bitcast(FP8X4),
-                            rhs_scale=v_sc[:, a * S + j0:a * S + j0 + JB],
+                            rhs_scale=v_sc[a][:, j0:j0 + JB],
                             start=(a == 0), stop=(a == A1 - 1))
                 nc.vector.tensor_tensor(
                     out=staged[:, jb * JB * PACK:(jb + 1) * JB * PACK].rearrange("p (c i t) -> p c t i", i=2, t=PACK),
@@ -122,7 +121,7 @@ def tile_list_item_equating_scores_kernel(tc, tab_words, tab_scales, tab2_words,
             sq[h, b] = quantise(staged, "sq")
 
         def scores(h, m):
-            acc = bank[MB * (1 - h) + m]
+            acc = bank[(A2 * (HALF // JB) + m) % BANKS]
             passes = [(q, b) for b in range(A2) for q in (hq, sq)]
             for n, (q, b) in enumerate(passes):
                 codes, scales = q[h, b]
@@ -145,31 +144,36 @@ def tile_list_item_equating_scores_kernel(tc, tab_words, tab_scales, tab2_words,
             nc.vector.tensor_tensor(out=page[m][:].indirect(idx3[:, entries(h)]), in0=y[h, m][:], in1=wg[h][:],
                                     op=ALU.mult)
 
-        for q in range(P // QUAD):
-            nc.vector.memset(tab_sc[q * QUAD:q * QUAD + TS0, :].bitcast(I32), 0)
+        nc.vector.memset(tab_sc[:].bitcast(I32), 0)
         nc.vector.memset(w_sc_raw[:].bitcast(I32), 0)
-        nc.vector.memset(v_sc[3 * QUAD:, :].bitcast(I32), 0)
+        for a in range(1, A1):
+            nc.vector.memset(v_sc[a][3 * QUAD:, :].bitcast(I32), 0)
         nc.vector.memset(tab2_sc[:].bitcast(I32), 0)
 
         nc.sync.dma_start(idx1[:], offs)
-        for q in range(P // QUAD):
-            nc.scalar.dma_start(out=tab_sc[q * QUAD + TS0:(q + 1) * QUAD, :].bitcast(I32),
-                                in_=tab_scales[:, LIVE * q:LIVE * (q + 1), :].bitcast(I32))
         nc.sync.dma_start(out=tab[0][:], in_=words(tab_words, 0))
+        for q in range(P // QUAD):
+            queue = nc.sync if q < 2 else nc.scalar
+            queue.dma_start(out=tab_sc[q * QUAD:q * QUAD + A1 * LIVE, :].bitcast(I32),
+                            in_=tab_scales[:, LIVE * q:LIVE * (q + 1), :].bitcast(I32))
         nc.sync.dma_start(out=tab[1][:], in_=words(tab_words, 1))
         for q in range(P // QUAD):
-            nc.gpsimd.dma_start(
+            nc.sync.dma_start(
                 out=w_sc_raw[q * QUAD:q * QUAD + LIVE, :].bitcast(I32).rearrange("r (a n) -> r a n", a=A1),
                 in_=w4_scales[:, LIVE * q:LIVE * (q + 1), :].bitcast(I32).rearrange("a r n -> r a n"))
         nc.sync.dma_start(out=w_raw[:].bitcast(I32).rearrange("p (a n) -> p a n", a=A1),
                           in_=w4_words.bitcast(I32).rearrange("a p n -> p a n"))
         nc.sync.dma_start(out=tab[2][:], in_=words(tab_words, 2))
+        fl[0, 0] = load_rows(floor_m, "fl", 0, 0)
+        nc.sync.dma_start(idx2[:], offs2)
+        for q in range(P // QUAD):
+            nc.gpsimd.dma_start(out=tab2_sc[q * QUAD:q * QUAD + A2 * LIVE, :].bitcast(I32),
+                                in_=tab2_scales[:, LIVE * q:LIVE * (q + 1), :].bitcast(I32))
 
-        nc.vector.tensor_copy(out=v_sc_packed[:], in_=tab_sc[:].indirect(idx1[:]))
-        for a in range(A1):
-            s0 = TS0 + LIVE * a
-            nc.scalar.dma_start(out=v_sc[:PLANE_ROWS, a * S:(a + 1) * S].bitcast(I32),
-                                in_=v_sc_packed[s0:s0 + PLANE_ROWS, :].bitcast(I32))
+        nc.vector.tensor_copy(out=v_sc[0][:], in_=tab_sc[:].indirect(idx1[:]))
+        for a in range(1, A1):
+            nc.sync.dma_start(out=v_sc[a][:PLANE_ROWS, :].bitcast(I32),
+                              in_=v_sc[0][LIVE * a:LIVE * a + PLANE_ROWS, :].bitcast(I32))
         for h in range(NH):
             for a in range(A1):
                 nc.vector.tensor_copy(out=v[a, h][:], in_=tab[a][:].bitcast(U32).indirect(idx1[:, entries(h)]))
@@ -182,29 +186,26 @@ def tile_list_item_equating_scores_kernel(tc, tab_words, tab_scales, tab2_words,
                 out=w[b][:].bitcast(U16).rearrange("p (a t m) -> p a t m", a=A1, t=PACK),
                 in_=w_raw[:].bitcast(U16).rearrange("p (a b m t) -> p b a t m", a=A1, b=A2, t=PACK)[:, b])
 
-        for b in range(A2):
-            fl[0, b] = load_rows(floor_m, "fl", 0, b)
+        nc.sync.dma_start(out=tab2[0][:], in_=words(tab2_words, 0))
+        fl[0, 1] = load_rows(floor_m, "fl", 0, 1)
         for b in range(A2):
             st[0, b] = load_rows(sit, "st", 0, b)
-        nc.sync.dma_start(idx2[:], offs2)
-        for q in range(P // QUAD):
-            nc.gpsimd.dma_start(out=tab2_sc[q * QUAD:q * QUAD + A2 * LIVE, :].bitcast(I32),
-                              in_=tab2_scales[:, LIVE * q:LIVE * (q + 1), :].bitcast(I32))
-        for a in range(A2):
-            nc.sync.dma_start(out=tab2[a][:], in_=words(tab2_words, a))
+        nc.sync.dma_start(out=tab2[1][:], in_=words(tab2_words, 1))
         nc.sync.dma_start(idx3[:], offs3)
         load_expo(0, 0)
-        load_expo(0, 1)
         load_wgo(0)
         load_page(0)
+        load_expo(0, 1)
 
+        nc.vector.tensor_copy(out=v2_sc[:], in_=tab2_sc[:].indirect(idx2[:]))
         for b in range(A2):
             features(0, b)
+        nc.vector.tensor_copy(out=v2[0][:], in_=tab2[0][:].bitcast(U32).indirect(idx2[:]))
         for b in range(A2):
             sitting(0, b)
-        nc.vector.tensor_copy(out=v2_sc[:], in_=tab2_sc[:].indirect(idx2[:]))
-        for a in range(A2):
-            nc.vector.tensor_copy(out=v2[a][:], in_=tab2[a][:].bitcast(U32).indirect(idx2[:]))
+        for m0, m1 in ((0, P), (P, S2)):
+            nc.vector.tensor_copy(out=v2[1][:, m0:m1],
+                                  in_=tab2[1][:].bitcast(U32).indirect(idx2[:, m0 // 16:m1 // 16]))
 
         load_expo(0, 2)
         load_expo(0, 3)

from contextlib import ExitStack

import concourse.mybir as mybir

K, H, T, S, T2, S2, T3 = 1536, 1024, 2048, 1024, 2048, 512, 2048
FLOPS = 2 * K * H * S + 2 * 2 * H * S2 * S

F32 = mybir.dt.float32
BF16 = mybir.dt.bfloat16
I32 = mybir.dt.int32
U32 = mybir.dt.uint32
U16 = mybir.dt.uint16
U8 = mybir.dt.uint8
FP8X4 = mybir.dt.float8_e4m3fn_x4
FP4X4 = mybir.dt.float4_e2m1fn_x4
ALU = mybir.AluOpType
ACT = mybir.ActivationFunctionType

P = 128
PACK = 4
KP = P * PACK
A1 = K // KP
A2 = H // KP
HALF = 512
NH = S // HALF
MB = S2 // P
JB = 128
QUAD = 32
LIVE = 4
BANKS = 6
PLANE_ROWS = 3 * QUAD + LIVE


def tile_list_item_equating_scores_kernel(tc, tab_words, tab_scales, tab2_words, tab2_scales,
                                                    w4_words, w4_scales, floor_m, sit, expo, page1, wgo,
                                                    offs, offs2, offs3, out):
    nc = tc.nc
    with ExitStack() as ctx:
        keep = ctx.enter_context(tc.tile_pool(name="keep", bufs=1))
        ring = ctx.enter_context(tc.tile_pool(name="ring", bufs=2))
        psum = ctx.enter_context(tc.psum_pool(name="psum", bufs=1))

        idx1 = keep.tile([P, S // 16], U16, name="idx1")
        idx2 = keep.tile([P, S2 // 16], U16, name="idx2")
        idx3 = keep.tile([P, S // 16], U16, name="idx3")
        tab = [keep.tile([P, T], I32, name="tab%d" % a) for a in range(A1)]
        tab2 = [keep.tile([P, T3], I32, name="tab2_%d" % a) for a in range(A2)]
        tab_sc = keep.tile([P, T], U8, name="tab_sc")
        tab2_sc = keep.tile([P, T3], U8, name="tab2_sc")
        v = {(a, h): keep.tile([P, HALF], U32, name="picked%d_%d" % (a, h), align_bytes=64)
             for a in range(A1) for h in range(NH)}
        v_sc = [keep.tile([P, S], U8, name="v_sc%d" % a, align_bytes=64) for a in range(A1)]
        v2 = [keep.tile([P, S2], U32, name="items%d" % a, align_bytes=64) for a in range(A2)]
        v2_sc = keep.tile([P, S2], U8, name="v2_sc", align_bytes=64)
        w_raw = keep.tile([P, A1 * 2 * H], U8, name="w_raw")
        w_sc_raw = keep.tile([P, A1 * H], U8, name="w_sc_raw")
        w = [keep.tile([P, A1 * 2 * KP], U8, name="w%d" % b, align_bytes=64) for b in range(A2)]
        w_sc = [keep.tile([P, A1 * KP], U8, name="w_sc%d" % b, align_bytes=64) for b in range(A2)]
        page = [keep.tile([P, T2], F32, name="page%d" % m) for m in range(MB)]
        wg = [keep.tile([P, HALF], F32, name="wg%d" % h) for h in range(NH)]
        bank = [psum.tile([P, HALF], F32, name="bank%d" % n) for n in range(BANKS)]
        ex = {}
        fl = {}
        st = {}
        hq = {}
        sq = {}
        y = {}

        def words(src, a):
            return src[a].rearrange("p t i -> p (t i)").bitcast(I32)

        def load_rows(src, tag, h, b):
            t = ring.tile([P, PACK, HALF], F32, name=tag, tag=tag)
            rows = src[b * KP:(b + 1) * KP, h * HALF:(h + 1) * HALF]
            nc.sync.dma_start(out=t[:], in_=rows.rearrange("(p t) j -> p t j", t=PACK))
            return t

        def load_expo(h, m):
            ex[h, m] = keep.tile([P, HALF], F32, name="ex%d_%d" % (h, m))
            nc.sync.dma_start(out=ex[h, m][:], in_=expo[m * P:(m + 1) * P, h * HALF:(h + 1) * HALF])

        def load_page(m):
            nc.sync.dma_start(out=page[m][:], in_=page1[m * P:(m + 1) * P, :])

        def load_wgo(h):
            nc.sync.dma_start(out=wg[h][:], in_=wgo[:, h * HALF:(h + 1) * HALF])

        def quantise(staged, tag):
            codes = ring.tile([P, HALF], U32, name=tag + "_codes", tag=tag + "_codes", bufs=4, align_bytes=64)
            scales = ring.tile([P, HALF], U8, name=tag + "_scales", tag=tag + "_scales", bufs=4, align_bytes=64)
            nc.vector.quantize_mx(out=codes[:].bitcast(FP8X4), scales=scales[:], in_=staged[:])
            return codes, scales

        def features(h, b):
            staged = ring.tile([P, HALF * PACK], BF16, name="h_bf", tag="h_bf", align_bytes=64)
            for jb in range(HALF // JB):
                j0 = h * HALF + jb * JB
                acc = bank[(b * (HALF // JB) + jb) % BANKS][:].rearrange("p (t j) -> p t j", t=PACK)
                for t in range(PACK):
                    for a in range(A1):
                        c0 = a * KP + t * P
                        nc.tensor.matmul_mx(
                            out=acc[:, t, :],
                            lhsT=w[b][:, 2 * c0:2 * (c0 + P)].bitcast(FP4X4),
                            lhsT_scale=w_sc[b][:, c0:c0 + P],
                            rhs=v[a, h][:, jb * JB:(jb + 1) * JB].bitcast(FP8X4),
                            rhs_scale=v_sc[a][:, j0:j0 + JB],
                            start=(a == 0), stop=(a == A1 - 1))
                nc.vector.tensor_tensor(
                    out=staged[:, jb * JB * PACK:(jb + 1) * JB * PACK].rearrange("p (c i t) -> p c t i", i=2, t=PACK),
                    in0=acc.rearrange("p t (c i) -> p c t i", i=2),
                    in1=fl[h, b][:, :, jb * JB:(jb + 1) * JB].rearrange("p t (c i) -> p c t i", i=2),
                    op=ALU.max)
            hq[h, b] = quantise(staged, "hq")

        def sitting(h, b):
            staged = ring.tile([P, HALF * PACK], BF16, name="s_bf", tag="s_bf", align_bytes=64)
            nc.scalar.copy(
                out=staged[:].rearrange("p (c i t) -> p c t i", i=2, t=PACK),
                in_=st[h, b][:].rearrange("p t (c i) -> p c t i", i=2))
            sq[h, b] = quantise(staged, "sq")

        def scores(h, m):
            acc = bank[(A2 * (HALF // JB) + m) % BANKS]
            passes = [(q, b) for b in range(A2) for q in (hq, sq)]
            for n, (q, b) in enumerate(passes):
                codes, scales = q[h, b]
                nc.tensor.matmul_mx(
                    out=acc[:],
                    lhsT=v2[b][:, m * P:(m + 1) * P].bitcast(FP8X4),
                    lhsT_scale=v2_sc[LIVE * b:, m * P:(m + 1) * P],
                    rhs=codes[:].bitcast(FP8X4),
                    rhs_scale=scales[:],
                    start=(n == 0), stop=(n == len(passes) - 1))
            z = ring.tile([P, HALF], F32, name="z", tag="z", bufs=3)
            nc.vector.tensor_tensor(out=z[:], in0=acc[:], in1=ex[h, m][:], op=ALU.mult)
            y[h, m] = keep.tile([P, HALF], F32, name="y%d_%d" % (h, m))
            nc.scalar.activation(out=y[h, m][:], in_=z[:], func=ACT.Tanh)

        def entries(h):
            return slice(h * HALF // 16, (h + 1) * HALF // 16)

        def put(h, m):
            nc.vector.tensor_tensor(out=page[m][:].indirect(idx3[:, entries(h)]), in0=y[h, m][:], in1=wg[h][:],
                                    op=ALU.mult)

        nc.vector.memset(tab_sc[:].bitcast(I32), 0)
        nc.vector.memset(w_sc_raw[:].bitcast(I32), 0)
        for a in range(1, A1):
            nc.vector.memset(v_sc[a][3 * QUAD:, :].bitcast(I32), 0)
        nc.vector.memset(tab2_sc[:].bitcast(I32), 0)

        nc.sync.dma_start(idx1[:], offs)
        nc.sync.dma_start(out=tab[0][:], in_=words(tab_words, 0))
        for q in range(P // QUAD):
            queue = nc.sync if q < 2 else nc.scalar
            queue.dma_start(out=tab_sc[q * QUAD:q * QUAD + A1 * LIVE, :].bitcast(I32),
                            in_=tab_scales[:, LIVE * q:LIVE * (q + 1), :].bitcast(I32))
        nc.sync.dma_start(out=tab[1][:], in_=words(tab_words, 1))
        for q in range(P // QUAD):
            nc.sync.dma_start(
                out=w_sc_raw[q * QUAD:q * QUAD + LIVE, :].bitcast(I32).rearrange("r (a n) -> r a n", a=A1),
                in_=w4_scales[:, LIVE * q:LIVE * (q + 1), :].bitcast(I32).rearrange("a r n -> r a n"))
        nc.sync.dma_start(out=w_raw[:].bitcast(I32).rearrange("p (a n) -> p a n", a=A1),
                          in_=w4_words.bitcast(I32).rearrange("a p n -> p a n"))
        nc.sync.dma_start(out=tab[2][:], in_=words(tab_words, 2))
        fl[0, 0] = load_rows(floor_m, "fl", 0, 0)
        nc.sync.dma_start(idx2[:], offs2)
        for q in range(P // QUAD):
            nc.gpsimd.dma_start(out=tab2_sc[q * QUAD:q * QUAD + A2 * LIVE, :].bitcast(I32),
                                in_=tab2_scales[:, LIVE * q:LIVE * (q + 1), :].bitcast(I32))

        nc.vector.tensor_copy(out=v_sc[0][:], in_=tab_sc[:].indirect(idx1[:]))
        for a in range(1, A1):
            nc.sync.dma_start(out=v_sc[a][:PLANE_ROWS, :].bitcast(I32),
                              in_=v_sc[0][LIVE * a:LIVE * a + PLANE_ROWS, :].bitcast(I32))
        for h in range(NH):
            for a in range(A1):
                nc.vector.tensor_copy(out=v[a, h][:], in_=tab[a][:].bitcast(U32).indirect(idx1[:, entries(h)]))

        for b in range(A2):
            nc.gpsimd.tensor_copy(
                out=w_sc[b][:].rearrange("p (a t m) -> p a t m", a=A1, t=PACK),
                in_=w_sc_raw[:].rearrange("p (a b m t) -> p b a t m", a=A1, b=A2, t=PACK)[:, b])
            nc.scalar.copy(
                out=w[b][:].bitcast(U16).rearrange("p (a t m) -> p a t m", a=A1, t=PACK),
                in_=w_raw[:].bitcast(U16).rearrange("p (a b m t) -> p b a t m", a=A1, b=A2, t=PACK)[:, b])

        nc.sync.dma_start(out=tab2[0][:], in_=words(tab2_words, 0))
        fl[0, 1] = load_rows(floor_m, "fl", 0, 1)
        for b in range(A2):
            st[0, b] = load_rows(sit, "st", 0, b)
        nc.sync.dma_start(out=tab2[1][:], in_=words(tab2_words, 1))
        nc.sync.dma_start(idx3[:], offs3)
        load_expo(0, 0)
        load_wgo(0)
        load_page(0)
        load_expo(0, 1)

        nc.vector.tensor_copy(out=v2_sc[:], in_=tab2_sc[:].indirect(idx2[:]))
        for b in range(A2):
            features(0, b)
        nc.vector.tensor_copy(out=v2[0][:], in_=tab2[0][:].bitcast(U32).indirect(idx2[:]))
        for b in range(A2):
            sitting(0, b)
        for m0, m1 in ((0, P), (P, S2)):
            nc.vector.tensor_copy(out=v2[1][:, m0:m1],
                                  in_=tab2[1][:].bitcast(U32).indirect(idx2[:, m0 // 16:m1 // 16]))

        load_expo(0, 2)
        load_expo(0, 3)
        for b in range(A2):
            load_page(1 + b)
            fl[1, b] = load_rows(floor_m, "fl", 1, b)
        for b in range(A2):
            st[1, b] = load_rows(sit, "st", 1, b)
        load_page(3)
        load_expo(1, 0)
        load_expo(1, 1)
        load_wgo(1)
        load_expo(1, 2)
        load_expo(1, 3)

        scores(0, 0)
        scores(0, 1)
        put(0, 0)
        scores(0, 2)
        scores(0, 3)
        for b in range(A2):
            put(0, 1 + b)
            features(1, b)
        for b in range(A2):
            sitting(1, b)
        put(0, MB - 1)
        scores(1, 0)
        for m in range(MB):
            if m + 1 < MB:
                scores(1, m + 1)
            put(1, m)
            nc.sync.dma_start(out=out[m * P:(m + 1) * P, :], in_=page[m][:])
